import numpy as np
import ml_dtypes


def mxq(x, axis, fmt="e4m3"):
    dtype, down = {"e4m3": (ml_dtypes.float8_e4m3fn, 7), "e5m2": (ml_dtypes.float8_e5m2, 14)}[fmt]
    v = np.moveaxis(np.asarray(x, np.float32).astype(ml_dtypes.bfloat16).astype(np.float64), axis, -1)
    blocks = v.reshape(v.shape[:-1] + (-1, 32))
    amax = np.abs(blocks).max(-1, keepdims=True)
    byte = np.maximum(np.where(amax > 0, np.frexp(amax)[1] - 1 + 127, 0) - down, 1)
    scale = np.exp2(byte - 127.0)
    codes = (blocks / scale).astype(np.float32).astype(dtype).astype(np.float64)
    return np.moveaxis((codes * scale).reshape(v.shape), -1, axis)


WIDE = False


def mx_kscale(k):
    if not WIDE:
        return np.ones(k)
    levels = np.array([10, -10, 5, -5, 0])
    if k % 512:
        return np.exp2(np.random.permutation(np.resize(levels, k // 32))).repeat(32)
    a = np.empty((k // 512, 16))
    for p in range(k // 512):
        a[p, :8] = np.random.permutation(np.resize(levels, 8))
        for g in range(8):
            far = levels[np.abs(levels - a[p, g]) >= 10]
            a[p, g + 8] = far[np.random.randint(len(far))]
    return np.exp2(a.ravel()).repeat(32)


BF16 = ml_dtypes.bfloat16


def bf(x):
    return np.asarray(x, np.float32).astype(BF16)


def f64(x):
    return np.asarray(x).astype(np.float64)

def planes(Y):
    n, m = Y.shape
    b = f64(bf(Y)).reshape(n // 32, 32, m)
    amax = np.abs(b).max(1)
    byte = np.clip(np.where(amax > 0, np.frexp(amax)[1] - 1 + 127 - 7, 1), 1, 254)
    codes = (b * np.exp2(127.0 - byte)[:, None, :]).reshape(n, m).astype(np.float32).astype(ml_dtypes.float8_e4m3fn).view(np.uint8)
    words = codes.reshape(n // 512, 128, 4, m).transpose(0, 1, 3, 2)
    return np.ascontiguousarray(words), np.ascontiguousarray(byte.astype(np.uint8).reshape(n // 512, 16, m))


H, S, M, D = 2, 512, 512, 512


def setup_inputs():
    s, t = mx_kscale(D), mx_kscale(M)
    a = np.linspace(0.7, 1.5, H)[:, None, None]
    return {
        "q": bf(np.random.standard_normal((H, S, D)) * s),
        "kp": bf(np.random.standard_normal((H, M, D)) / s),
        "vp": bf(np.random.standard_normal((H, M, D)) / t[:, None]),
        "kn": bf(np.random.standard_normal((H, M, D)) / s),
        "vn": bf(np.random.standard_normal((H, M, D)) * a / t[:, None]),
        "g": bf(np.random.standard_normal(M) * t),
    }


def gated_attention(qq, k, v, g):
    kt = mxq(f64(k).transpose(0, 2, 1), 1, "e4m3")
    logits = (qq @ kt) / np.sqrt(D)
    e = np.exp(logits - logits.max(-1, keepdims=True))
    probs = e / e.sum(-1, keepdims=True) * f64(g)[None, None, :] * np.sqrt(M)
    return mxq(probs, 2, "e4m3") @ mxq(f64(v), 1, "e4m3")


def core(q, kp, vp, kn, vn, g):
    qq = mxq(f64(q), 2, "e4m3")
    zp = gated_attention(qq, kp, vp, g)
    zn = gated_attention(qq, kn, vn, g)
    zt = 2.0 * zp - zn
    r = np.sum(np.abs(zt), axis=-1) / (np.sum(np.abs(zp), axis=-1) + 1e-6)
    factor = np.minimum(r, 2.2) / (r + 1e-6)
    zh = zt * factor[..., None]
    return 0.7 * zh + 0.3 * zp


def reference(q, kp, vp, kn, vn, g):
    R_out = core(q, kp, vp, kn, vn, g)
    words, scales = planes(np.moveaxis(R_out, 1, 0).reshape(512, -1))
    return R_out, words, scales

@@ -1,0 +1,483 @@
+from contextlib import ExitStack
+import math
+
+import concourse.mybir as mybir
+from concourse.masks import make_identity
+
+H, S, M, D = 2, 512, 512, 512
+P = 128
+PACK = 4
+FLOPS = 2 * 4 * H * S * M * D
+
+F32 = mybir.dt.float32
+BF16 = mybir.dt.bfloat16
+U32 = mybir.dt.uint32
+I32 = mybir.dt.int32
+U8 = mybir.dt.uint8
+FP8X4 = mybir.dt.float8_e4m3fn_x4
+ALU = mybir.AluOpType
+ACT = mybir.ActivationFunctionType
+
+EPS = 1e-6
+CLIP = 2.2
+INV_SQRT_D = 1.0 / math.sqrt(D)
+SQRT_M = math.sqrt(M)
+PAIRS = H * PACK
+
+
+def tile_normalizedattentionguidancemerge_x1_kernel(tc, q, kp, vp, kn, vn, g, out_0, out_1, out_2):
+    nc = tc.nc
+    with ExitStack() as ctx:
+        keep = ctx.enter_context(tc.tile_pool(name="keep", bufs=1))
+        ring = ctx.enter_context(tc.tile_pool(name="ring", bufs=2))
+        psum = ctx.enter_context(tc.psum_pool(name="psum", bufs=1))
+        ctx.enter_context(tc.manual_schedule())
+
+        def persist(label, shape, dtype):
+            return keep.tile(shape, dtype, name=label, tag=label, align_bytes=256)
+
+        raw = {}
+        for h in range(H):
+            for label in ("q", "kp", "kn", "vp", "vn"):
+                raw[label, h] = persist("raw_%s%d" % (label, h), [P, PACK, D], BF16)
+        dram = {"q": q, "kp": kp, "kn": kn, "vp": vp, "vn": vn}
+
+        def load(label, h, lo, hi):
+            src = dram[label][h].rearrange("(p t) d -> p t d", t=PACK)
+            nc.sync.dma_start(out=raw[label, h][:, lo:hi, :], in_=src[:, lo:hi, :])
+
+        g_rows = persist("g_rows", [P, M], BF16)
+        nc.vector.memset(g_rows[:], 0.0)
+        zeros = persist("zeros", [P, P], F32)
+        nc.vector.memset(zeros[:], 0.0)
+        nc.scalar.dma_start(out=g_rows[0:1, :], in_=g.rearrange("(o m) -> o m", o=1))
+        load("kp", 0, 0, 2)
+        load("q", 0, 0, 2)
+        load("kp", 0, 2, 4)
+        load("kn", 0, 0, 4)
+        load("vp", 0, 0, 4)
+        load("q", 0, 2, 4)
+        load("vn", 0, 0, 4)
+        for label in ("q", "kp", "kn", "vp", "vn"):
+            load(label, 1, 0, 4)
+
+        ident = persist("ident", [P, P], F32)
+        make_identity(nc, ident[:])
+        ones = persist("ones", [P, P], BF16)
+        nc.scalar.activation(out=ones[:], in_=zeros[:], func=ACT.Exp)
+
+        codes = {}
+        scales = {}
+        for h in range(H):
+            for label in ("q", "kp", "kn", "vp", "vn"):
+                codes[label, h] = persist("c_%s%d" % (label, h), [P, D], U32)
+                scales[label, h] = persist("s_%s%d" % (label, h), [P, D], U8)
+
+        def quantize(out, plane, in_):
+            nc.vector.quantize_mx(out=out.bitcast(FP8X4), scales=plane, in_=in_)
+
+        staged = {}
+
+        def turn(label, h, half):
+            words = raw[label, h][:].bitcast(F32)
+            bank = psum.tile([P, 4, P], F32, name="bank", tag="tp", bufs=3)
+            for e in range(2):
+                for w in range(2):
+                    nc.tensor.transpose(bank[:, 2 * e + w, :], words[:, 2 * half + e, w:256:2], ident[:])
+            staged[label, h, half] = bank
+
+        def untangle(label, h, half, copy):
+            bank = staged[label, h, half]
+            group = ring.tile([P, 2 * D], BF16, name="group", tag="group", bufs=4, align_bytes=256)
+            dst = group[:].bitcast(F32)
+            if label == "q":
+                copy(out=dst.rearrange("p (e m w) -> p e m w", e=2, w=2), in_=bank[:].rearrange("p (e w) m -> p e m w", w=2))
+            else:
+                copy(out=dst.rearrange("p (m s) -> p m s", s=4), in_=bank[:].rearrange("p s m -> p m s"))
+            staged[label, h, half] = group
+
+        def quant_half(label, h, half):
+            cols = slice(256 * half, 256 * half + 256)
+            quantize(codes[label, h][:, cols], scales[label, h][:, cols], staged[label, h, half][:])
+
+        def v_group(label, h):
+            t = ring.tile([P, D, PACK], BF16, name="vgroup", tag="vgroup", bufs=4, align_bytes=256)
+            staged[label, h] = t
+
+        def v_inter(eng, label, h, part, parts):
+            n = D // parts
+            cols = slice(part * n, part * n + n)
+            dst = staged[label, h][:, cols, :]
+            src = raw[label, h][:, :, cols].rearrange("p t d -> p d t")
+            if eng is nc.gpsimd:
+                nc.gpsimd.tensor_scalar(out=dst, in0=src, scalar1=1.0, scalar2=0.0, op0=ALU.mult, op1=ALU.add)
+            else:
+                nc.vector.tensor_copy(out=dst, in_=src)
+
+        def v_quant(label, h):
+            quantize(codes[label, h][:], scales[label, h][:], staged[label, h][:].rearrange("p d t -> p (d t)"))
+
+        K_OF = ("kp", "kn")
+        V_OF = ("vp", "vn")
+        st = {}
+
+        def logits(i, b):
+            h, t = divmod(i, PACK)
+            cols = slice(P * t, P * t + P)
+            lg = psum.tile([P, M], F32, name="lg%d" % b, tag="lg%d" % b, bufs=1)
+            nc.tensor.matmul_mx(
+                out=lg[:],
+                lhsT=codes["q", h][:, cols].bitcast(FP8X4),
+                lhsT_scale=scales["q", h][:, cols],
+                rhs=codes[K_OF[b], h][:].bitcast(FP8X4),
+                rhs_scale=scales[K_OF[b], h][:],
+                start=True,
+                stop=True,
+            )
+            st[i, "lg", b] = lg
+
+        def minpass(i, b):
+            if b == 0:
+                st[i, "neg"] = ring.tile([P, 2, M], F32, name="neg", tag="neg", bufs=2)
+                st[i, "nb"] = ring.tile([P, 2], F32, name="nb", tag="nb", bufs=3)
+            nc.vector.tensor_scalar(
+                out=st[i, "neg"][:, b, :],
+                in0=st[i, "lg", b][:],
+                scalar1=-INV_SQRT_D,
+                scalar2=None,
+                op0=ALU.mult,
+                op1=ALU.min,
+                accum_out=st[i, "nb"][:, b : b + 1],
+            )
+
+        def denominators(i):
+            if (i, "den") not in st:
+                st[i, "den"] = ring.tile([P, 3], F32, name="den", tag="den", bufs=4)
+
+        def expo(i, b):
+            if b == 0:
+                st[i, "e"] = ring.tile([P, 2, M], F32, name="e", tag="e", bufs=2)
+                denominators(i)
+            nc.scalar.activation(
+                out=st[i, "e"][:, b, :],
+                in_=st[i, "neg"][:, b, :],
+                func=ACT.Exp,
+                scale=-1.0,
+                bias=st[i, "nb"][:, b : b + 1],
+                accum_out=st[i, "den"][:, b : b + 1],
+            )
+
+        def recip(i):
+            lo, hi = (0 if i < PAIRS else 2), (3 if i >= 2 else 2)
+            st[i, "rs"] = ring.tile([P, 3], F32, name="rs", tag="rs", bufs=3)
+            nc.vector.reciprocal(out=st[i, "rs"][:, lo:hi], in_=st[i, "den"][:, lo:hi])
+
+        def probs(i, b):
+            if b == 0:
+                st[i, "p"] = ring.tile([P, 2, M], BF16, name="pr", tag="pr", bufs=2, align_bytes=256)
+            nc.vector.scalar_tensor_tensor(
+                out=st[i, "p"][:, b, :],
+                in0=st[i, "e"][:, b, :],
+                scalar=st[i, "rs"][:, b : b + 1],
+                in1=g_all[b][:],
+                op0=ALU.mult,
+                op1=ALU.mult,
+            )
+
+        def turn_branch(i, b):
+            words = st[i, "p"][:].bitcast(F32)
+            bank = psum.tile([P, 4, P], F32, name="bank", tag="tp", bufs=3)
+            for u in range(2):
+                nc.tensor.transpose(bank[:, u, :], words[:, b, P * u : P * u + P], ident[:])
+            st[i, "bank", b] = bank
+
+        def copy_branch(i, b, copy):
+            if b == 0:
+                st[i, "pg"] = ring.tile([P, 2 * M], BF16, name="pgroup", tag="pgroup", bufs=2, align_bytes=256)
+            dst = st[i, "pg"][:, M * b : M * b + M].bitcast(F32).rearrange("p (s u) -> p s u", u=2)
+            copy(out=dst, in_=st[i, "bank", b][:, 0:2, :].rearrange("p u s -> p s u"))
+
+        def quant_branch(i, b):
+            if b == 0:
+                st[i, "pc"] = ring.tile([P, 2 * P], U32, name="pcodes", tag="pcodes", bufs=2, align_bytes=256)
+                st[i, "ps"] = ring.tile([P, 2 * P], U8, name="pscales", tag="pscales", bufs=2, align_bytes=256)
+            cols = slice(P * b, P * b + P)
+            quantize(st[i, "pc"][:, cols], st[i, "ps"][:, cols], st[i, "pg"][:, M * b : M * b + M])
+
+        def turn_probs(i):
+            words = st[i, "p"][:].bitcast(F32)
+            bank = psum.tile([P, 4, P], F32, name="bank", tag="tp", bufs=3)
+            for b in range(2):
+                for u in range(2):
+                    nc.tensor.transpose(bank[:, 2 * b + u, :], words[:, b, P * u : P * u + P], ident[:])
+            st[i, "bank"] = bank
+
+        def copy_probs(i):
+            group = ring.tile([P, 2 * M], BF16, name="pgroup", tag="pgroup", bufs=2, align_bytes=256)
+            dst = group[:].bitcast(F32).rearrange("p (b s u) -> p b s u", b=2, u=2)
+            nc.scalar.copy(out=dst, in_=st[i, "bank"][:].rearrange("p (b u) s -> p b s u", u=2))
+            st[i, "pg"] = group
+
+        def quant_probs(i):
+            c = ring.tile([P, 2 * P], U32, name="pcodes", tag="pcodes", bufs=2, align_bytes=256)
+            s = ring.tile([P, 2 * P], U8, name="pscales", tag="pscales", bufs=2, align_bytes=256)
+            quantize(c[:], s[:], st[i, "pg"][:])
+            st[i, "pc"], st[i, "ps"] = c, s
+
+        def values(i):
+            h = i // PACK
+
+            def one(out, b, start, stop):
+                cols = slice(P * b, P * b + P)
+                nc.tensor.matmul_mx(
+                    out=out[:],
+                    lhsT=st[i, "pc"][:, cols].bitcast(FP8X4),
+                    lhsT_scale=st[i, "ps"][:, cols],
+                    rhs=codes[V_OF[b], h][:].bitcast(FP8X4),
+                    rhs_scale=scales[V_OF[b], h][:],
+                    start=start,
+                    stop=stop,
+                )
+
+            zp = psum.tile([P, D], F32, name="zp", tag="zp", bufs=1)
+            zt = psum.tile([P, D], F32, name="zt", tag="zt", bufs=2)
+            one(zp, 0, True, True)
+            one(zt, 0, True, False)
+            one(zt, 0, False, False)
+            one(zt, 1, False, True)
+            st[i, "zp"], st[i, "zt"] = zp, zt
+
+        def abs_sum(i, which):
+            if which == "zp":
+                st[i, "l1"] = ring.tile([P, 2], F32, name="l1", tag="l1", bufs=3)
+            junk = ring.tile([P, D], BF16, name="junk", tag="junk", bufs=2)
+            col = 0 if which == "zp" else 1
+            nc.scalar.activation(out=junk[:], in_=st[i, which][:], func=ACT.Abs, accum_out=st[i, "l1"][:, col : col + 1])
+
+        def keep_zp(i, last):
+            st[i, "zp3"] = ring.tile([P, D], F32, name="zp3", tag="zp3", bufs=3)
+            if last:
+                nc.vector.tensor_scalar(out=st[i, "zp3"][:], in0=st[i, "zp"][:], scalar1=0.3, scalar2=None, op0=ALU.mult)
+            else:
+                nc.scalar.activation(out=st[i, "zp3"][:], in_=st[i, "zp"][:], func=ACT.Copy, scale=0.3)
+
+        def small_ops(i, eng):
+            w = ring.tile([P, 8], F32, name="w", tag="w", bufs=3)
+            st[i, "w"] = w
+            sp, s_t = st[i, "l1"][:, 0:1], st[i, "l1"][:, 1:2]
+            eng.tensor_scalar(out=w[:, 0:1], in0=sp, scalar1=EPS, scalar2=CLIP, op0=ALU.add, op1=ALU.mult)
+            denominators(i + 2)
+            eng.tensor_scalar(out=st[i + 2, "den"][:, 2:3], in0=w[:, 0:1], scalar1=EPS / CLIP, scalar2=s_t, op0=ALU.mult, op1=ALU.add)
+            eng.tensor_scalar(out=w[:, 2:3], in0=w[:, 0:1], scalar1=s_t, scalar2=0.7, op0=ALU.min, op1=ALU.mult)
+
+        def factor(i, eng):
+            a = ring.tile([P, 1], F32, name="a", tag="a", bufs=3)
+            eng.tensor_tensor(out=a[:], in0=st[i, "w"][:, 2:3], in1=st[i + 2, "rs"][:, 2:3], op=ALU.mult)
+            st[i, "a"] = a
+
+        ob = {}
+
+        def blend(i):
+            h, t = divmod(i, PACK)
+            if t == 0:
+                ob[h] = persist("ob%d" % h, [P, PACK, D], F32)
+            nc.vector.scalar_tensor_tensor(
+                out=ob[h][:, t, :], in0=st[i, "zt"][:], scalar=st[i, "a"][:], in1=st[i, "zp3"][:], op0=ALU.mult, op1=ALU.add
+            )
+            dst = out_0[h].rearrange("(p t) d -> p t d", t=PACK)
+            nc.sync.dma_start(out=dst[:, t, :], in_=ob[h][:, t, :])
+
+        def planes_group(h):
+            staged["ob", h] = persist("og%d" % h, [P, D, PACK], BF16)
+            codes["ob", h] = persist("oc%d" % h, [P, D], U32)
+            scales["ob", h] = persist("os%d" % h, [P, D], U8)
+
+        def planes_inter(h, lo, hi, eng):
+            dst = staged["ob", h][:, lo:hi, :]
+            src = ob[h][:, :, lo:hi].rearrange("p t d -> p d t")
+            if eng is nc.scalar:
+                nc.scalar.copy(out=dst, in_=src)
+            elif eng is nc.gpsimd:
+                nc.gpsimd.tensor_scalar(out=dst, in0=src, scalar1=1.0, scalar2=0.0, op0=ALU.mult, op1=ALU.add)
+            else:
+                nc.vector.tensor_copy(out=dst, in_=src)
+
+        def planes_quant(h, lo, hi):
+            quantize(codes["ob", h][:, lo:hi], scales["ob", h][:, lo:hi], staged["ob", h][:, lo:hi, :].rearrange("p d t -> p (d t)"))
+
+        def planes_store(h, lo, hi):
+            a, b = h * D + lo, h * D + hi
+            nc.sync.dma_start(out=out_1[0, :, a:b, :].rearrange("p d t -> p (d t)").bitcast(I32), in_=codes["ob", h][:, lo:hi].bitcast(I32))
+
+        def scales_store(h):
+            for quad in range(4):
+                nc.sync.dma_start(
+                    out=out_2[0, 4 * quad : 4 * quad + 4, h * D : h * D + D].bitcast(I32),
+                    in_=scales["ob", h][32 * quad : 32 * quad + 4, :].bitcast(I32),
+                )
+
+        s_copy = nc.scalar.copy
+        v_copy = nc.vector.tensor_copy
+        g_bank = psum.tile([P, M], F32, name="zt", tag="zt", bufs=2)
+        nc.tensor.matmul(out=g_bank[:], lhsT=ones[:], rhs=g_rows[:], start=True, stop=True)
+        g_all = []
+        for b, factor_b in enumerate((SQRT_M, -SQRT_M)):
+            gt = persist("g%d" % b, [P, M], F32)
+            nc.vector.tensor_scalar(
+                out=gt[:].rearrange("p (u m e) -> p u m e", u=2, e=2),
+                in0=g_bank[:].rearrange("p (m u e) -> p u m e", u=2, e=2),
+                scalar1=factor_b,
+                scalar2=None,
+                op0=ALU.mult,
+            )
+            g_all.append(gt)
+        v_group("vp", 0)
+        turn("kp", 0, 0)
+        untangle("kp", 0, 0, s_copy)
+        turn("q", 0, 0)
+        untangle("q", 0, 0, s_copy)
+        turn("kp", 0, 1)
+        untangle("kp", 0, 1, s_copy)
+        quant_half("kp", 0, 0)
+        quant_half("q", 0, 0)
+        quant_half("kp", 0, 1)
+        turn("kn", 0, 0)
+        untangle("kn", 0, 0, s_copy)
+        turn("kn", 0, 1)
+        untangle("kn", 0, 1, s_copy)
+        logits(0, 0)
+        v_inter(nc.vector, "vp", 0, 0, 2)
+        turn("q", 0, 1)
+        untangle("q", 0, 1, s_copy)
+        minpass(0, 0)
+        logits(1, 0)
+        quant_half("kn", 0, 0)
+        quant_half("kn", 0, 1)
+        logits(0, 1)
+        expo(0, 0)
+        v_inter(nc.vector, "vp", 0, 1, 2)
+        minpass(0, 1)
+        logits(1, 1)
+        expo(0, 1)
+        quant_half("q", 0, 1)
+        v_group("vn", 0)
+        for part in range(4):
+            v_inter(nc.gpsimd, "vn", 0, part, 4)
+        for label in ("vp", "vn"):
+            v_group(label, 1)
+
+        turns = {0: (("q", 0), ("q", 1), ("kp", 0)), 1: (("kp", 1), ("kn", 0), ("kn", 1))}
+        vparts = {1: (("vp", 0), ("vp", 1)), 2: (("vp", 2), ("vp", 3)), 3: (("vn", 0), ("vn", 1)), 4: (("vn", 2), ("vn", 3))}
+        on_v = {(1, 2)}
+
+        def side_turn(i, k):
+            if i in turns:
+                turn(turns[i][k][0], 1, turns[i][k][1])
+
+        def side_copy(i, k):
+            if i in turns:
+                untangle(turns[i][k][0], 1, turns[i][k][1], v_copy if (i, k) in on_v else s_copy)
+
+        def side_quant(i, k):
+            if i in turns:
+                quant_half(turns[i][k][0], 1, turns[i][k][1])
+
+        for i in range(PAIRS - 1):
+            nxt, prev = i + 1, i - 1
+            side_turn(i, 0)
+            side_copy(i, 0)
+            minpass(nxt, 0)
+            if i + 2 < PAIRS:
+                logits(i + 2, 0)
+            expo(nxt, 0)
+            minpass(nxt, 1)
+            if i + 2 < PAIRS:
+                logits(i + 2, 1)
+            side_turn(i, 1)
+            if i == 1:
+                side_turn(i, 2)
+            expo(nxt, 1)
+            side_copy(i, 1)
+            if i == 0:
+                v_quant("vp", 0)
+            if i == 5:
+                v_quant("vn", 1)
+            recip(i)
+            if prev >= 0:
+                quant_probs(prev)
+                values(prev)
+            if i - 2 >= 0:
+                factor(i - 2, nc.gpsimd)
+            for label, part in vparts.get(i, ()):
+                v_inter(nc.gpsimd, label, 1, part, 4)
+            if i == 6:
+                planes_group(0)
+                for part in range(2):
+                    planes_inter(0, 128 * part, 128 * part + 128, nc.gpsimd)
+            side_quant(i, 0)
+            probs(i, 0)
+            probs(i, 1)
+            if i == 0:
+                side_turn(i, 2)
+            if prev >= 0:
+                abs_sum(prev, "zp")
+            if i == 1:
+                side_copy(i, 2)
+            if prev >= 0:
+                abs_sum(prev, "zt")
+                small_ops(prev, nc.gpsimd)
+            turn_probs(i)
+            side_quant(i, 1)
+            if i == 0:
+                side_copy(i, 2)
+                v_quant("vn", 0)
+            copy_probs(i)
+            if prev >= 0:
+                keep_zp(prev, False)
+            if i - 2 >= 0:
+                blend(i - 2)
+            side_quant(i, 2)
+            if i == 3:
+                v_quant("vp", 1)
+
+        i = PAIRS - 1
+        recip(i)
+        factor(i - 2, nc.gpsimd)
+        for part in range(2, 4):
+            planes_inter(0, 128 * part, 128 * part + 128, nc.gpsimd)
+        probs(i, 0)
+        turn_branch(i, 0)
+        quant_probs(i - 1)
+        values(i - 1)
+        probs(i, 1)
+        turn_branch(i, 1)
+        copy_branch(i, 0, s_copy)
+        abs_sum(i - 1, "zp")
+        copy_branch(i, 1, s_copy)
+        abs_sum(i - 1, "zt")
+        blend(i - 2)
+        quant_branch(i, 0)
+        keep_zp(i - 1, True)
+        small_ops(i - 1, nc.gpsimd)
+        quant_branch(i, 1)
+        values(i)
+        recip(i + 1)
+        factor(i - 1, nc.gpsimd)
+        planes_quant(0, 0, D)
+        planes_store(0, 0, D)
+        scales_store(0)
+        blend(i - 1)
+        abs_sum(i, "zp")
+        keep_zp(i, True)
+        abs_sum(i, "zt")
+        small_ops(i, nc.vector)
+        recip(i + 2)
+        factor(i, nc.vector)
+        blend(i)
+        planes_group(1)
+        planes_inter(1, 0, 352, nc.vector)
+        planes_inter(1, 352, D, nc.scalar)
+        planes_quant(1, 0, 256)
+        planes_quant(1, 256, D)
+        planes_store(1, 0, D)
+        scales_store(1)

@@ -50,7 +50,9 @@ def tile_normalizedattentionguidancemerge_x1_kernel(tc, q, kp, vp, kn, vn, g, ou
         nc.vector.memset(g_rows[:], 0.0)
         zeros = persist("zeros", [P, P], F32)
         nc.vector.memset(zeros[:], 0.0)
-        nc.scalar.dma_start(out=g_rows[0:1, :], in_=g.rearrange("(o m) -> o m", o=1))
+        g_one = persist("g_one", [1, M], BF16)
+        nc.sync.dma_start(out=g_one[:], in_=g.rearrange("(o m) -> o m", o=1))
+        nc.vector.tensor_copy(out=g_rows[0:1, :], in_=g_one[:])
         load("kp", 0, 0, 2)
         load("q", 0, 0, 2)
         load("kp", 0, 2, 4)
@@ -109,10 +111,7 @@ def tile_normalizedattentionguidancemerge_x1_kernel(tc, q, kp, vp, kn, vn, g, ou
             cols = slice(part * n, part * n + n)
             dst = staged[label, h][:, cols, :]
             src = raw[label, h][:, :, cols].rearrange("p t d -> p d t")
-            if eng is nc.gpsimd:
-                nc.gpsimd.tensor_scalar(out=dst, in0=src, scalar1=1.0, scalar2=0.0, op0=ALU.mult, op1=ALU.add)
-            else:
-                nc.vector.tensor_copy(out=dst, in_=src)
+            eng(out=dst, in_=src)
 
         def v_quant(label, h):
             quantize(codes[label, h][:], scales[label, h][:], staged[label, h][:].rearrange("p d t -> p (d t)"))
@@ -167,9 +166,9 @@ def tile_normalizedattentionguidancemerge_x1_kernel(tc, q, kp, vp, kn, vn, g, ou
                 accum_out=st[i, "den"][:, b : b + 1],
             )
 
-        def recip(i):
-            lo, hi = (0 if i < PAIRS else 2), (3 if i >= 2 else 2)
-            st[i, "rs"] = ring.tile([P, 3], F32, name="rs", tag="rs", bufs=3)
+        def recip(i, lo, hi):
+            if (i, "rs") not in st:
+                st[i, "rs"] = ring.tile([P, 3], F32, name="rs", tag="rs", bufs=3)
             nc.vector.reciprocal(out=st[i, "rs"][:, lo:hi], in_=st[i, "den"][:, lo:hi])
 
         def probs(i, b):
@@ -254,26 +253,32 @@ def tile_normalizedattentionguidancemerge_x1_kernel(tc, q, kp, vp, kn, vn, g, ou
             col = 0 if which == "zp" else 1
             nc.scalar.activation(out=junk[:], in_=st[i, which][:], func=ACT.Abs, accum_out=st[i, "l1"][:, col : col + 1])
 
-        def keep_zp(i, last):
+        def keep_zp(i, on_vector):
             st[i, "zp3"] = ring.tile([P, D], F32, name="zp3", tag="zp3", bufs=3)
-            if last:
+            if on_vector:
                 nc.vector.tensor_scalar(out=st[i, "zp3"][:], in0=st[i, "zp"][:], scalar1=0.3, scalar2=None, op0=ALU.mult)
             else:
                 nc.scalar.activation(out=st[i, "zp3"][:], in_=st[i, "zp"][:], func=ACT.Copy, scale=0.3)
 
-        def small_ops(i, eng):
-            w = ring.tile([P, 8], F32, name="w", tag="w", bufs=3)
-            st[i, "w"] = w
-            sp, s_t = st[i, "l1"][:, 0:1], st[i, "l1"][:, 1:2]
-            eng.tensor_scalar(out=w[:, 0:1], in0=sp, scalar1=EPS, scalar2=CLIP, op0=ALU.add, op1=ALU.mult)
-            denominators(i + 2)
-            eng.tensor_scalar(out=st[i + 2, "den"][:, 2:3], in0=w[:, 0:1], scalar1=EPS / CLIP, scalar2=s_t, op0=ALU.mult, op1=ALU.add)
-            eng.tensor_scalar(out=w[:, 2:3], in0=w[:, 0:1], scalar1=s_t, scalar2=0.7, op0=ALU.min, op1=ALU.mult)
+        def bound(i):
+            st[i, "w"] = ring.tile([P, 1], F32, name="w", tag="w", bufs=3)
+            nc.scalar.activation(out=st[i, "w"][:], in_=st[i, "l1"][:, 0:1], func=ACT.Copy, scale=CLIP, bias=CLIP * EPS)
 
-        def factor(i, eng):
-            a = ring.tile([P, 1], F32, name="a", tag="a", bufs=3)
-            eng.tensor_tensor(out=a[:], in0=st[i, "w"][:, 2:3], in1=st[i + 2, "rs"][:, 2:3], op=ALU.mult)
-            st[i, "a"] = a
+        def norm(i):
+            denominators(i + 2)
+            nc.scalar.activation(
+                out=st[i + 2, "den"][:, 2:3], in_=st[i, "w"][:], func=ACT.Identity, scale=EPS / CLIP, bias=st[i, "l1"][:, 1:2]
+            )
+
+        def clipped(i):
+            st[i, "num"] = ring.tile([P, 1], F32, name="num", tag="num", bufs=3)
+            nc.vector.tensor_scalar(
+                out=st[i, "num"][:], in0=st[i, "w"][:], scalar1=st[i, "l1"][:, 1:2], scalar2=0.7, op0=ALU.min, op1=ALU.mult
+            )
+
+        def factor(i):
+            st[i, "a"] = ring.tile([P, 1], F32, name="a", tag="a", bufs=3)
+            nc.vector.tensor_tensor(out=st[i, "a"][:], in0=st[i, "num"][:], in1=st[i + 2, "rs"][:, 2:3], op=ALU.mult)
 
         ob = {}
 
@@ -295,12 +300,7 @@ def tile_normalizedattentionguidancemerge_x1_kernel(tc, q, kp, vp, kn, vn, g, ou
         def planes_inter(h, lo, hi, eng):
             dst = staged["ob", h][:, lo:hi, :]
             src = ob[h][:, :, lo:hi].rearrange("p t d -> p d t")
-            if eng is nc.scalar:
-                nc.scalar.copy(out=dst, in_=src)
-            elif eng is nc.gpsimd:
-                nc.gpsimd.tensor_scalar(out=dst, in0=src, scalar1=1.0, scalar2=0.0, op0=ALU.mult, op1=ALU.add)
-            else:
-                nc.vector.tensor_copy(out=dst, in_=src)
+            eng(out=dst, in_=src)
 
         def planes_quant(h, lo, hi):
             quantize(codes["ob", h][:, lo:hi], scales["ob", h][:, lo:hi], staged["ob", h][:, lo:hi, :].rearrange("p d t -> p (d t)"))
@@ -346,7 +346,7 @@ def tile_normalizedattentionguidancemerge_x1_kernel(tc, q, kp, vp, kn, vn, g, ou
         turn("kn", 0, 1)
         untangle("kn", 0, 1, s_copy)
         logits(0, 0)
-        v_inter(nc.vector, "vp", 0, 0, 2)
+        v_inter(v_copy, "vp", 0, 0, 2)
         turn("q", 0, 1)
         untangle("q", 0, 1, s_copy)
         minpass(0, 0)
@@ -355,20 +355,17 @@ def tile_normalizedattentionguidancemerge_x1_kernel(tc, q, kp, vp, kn, vn, g, ou
         quant_half("kn", 0, 1)
         logits(0, 1)
         expo(0, 0)
-        v_inter(nc.vector, "vp", 0, 1, 2)
+        v_inter(v_copy, "vp", 0, 1, 2)
         minpass(0, 1)
         logits(1, 1)
         expo(0, 1)
         quant_half("q", 0, 1)
         v_group("vn", 0)
-        for part in range(4):
-            v_inter(nc.gpsimd, "vn", 0, part, 4)
         for label in ("vp", "vn"):
             v_group(label, 1)
 
         turns = {0: (("q", 0), ("q", 1), ("kp", 0)), 1: (("kp", 1), ("kn", 0), ("kn", 1))}
-        vparts = {1: (("vp", 0), ("vp", 1)), 2: (("vp", 2), ("vp", 3)), 3: (("vn", 0), ("vn", 1)), 4: (("vn", 2), ("vn", 3))}
-        on_v = {(1, 2)}
+        sparts = {2: (0,), 3: (1,)}
 
         def side_turn(i, k):
             if i in turns:
@@ -376,7 +373,7 @@ def tile_normalizedattentionguidancemerge_x1_kernel(tc, q, kp, vp, kn, vn, g, ou
 
         def side_copy(i, k):
             if i in turns:
-                untangle(turns[i][k][0], 1, turns[i][k][1], v_copy if (i, k) in on_v else s_copy)
+                untangle(turns[i][k][0], 1, turns[i][k][1], s_copy)
 
         def side_quant(i, k):
             if i in turns:
@@ -400,83 +397,97 @@ def tile_normalizedattentionguidancemerge_x1_kernel(tc, q, kp, vp, kn, vn, g, ou
             side_copy(i, 1)
             if i == 0:
                 v_quant("vp", 0)
+            recip(i, 0, 3 if i >= 2 else 2)
+            if i >= 2:
+                clipped(i - 2)
+            if i == 1:
+                v_quant("vn", 0)
             if i == 5:
                 v_quant("vn", 1)
-            recip(i)
             if prev >= 0:
                 quant_probs(prev)
                 values(prev)
-            if i - 2 >= 0:
-                factor(i - 2, nc.gpsimd)
-            for label, part in vparts.get(i, ()):
-                v_inter(nc.gpsimd, label, 1, part, 4)
-            if i == 6:
-                planes_group(0)
-                for part in range(2):
-                    planes_inter(0, 128 * part, 128 * part + 128, nc.gpsimd)
             side_quant(i, 0)
+            if i == 4:
+                v_quant("vp", 1)
             probs(i, 0)
+            if i >= 2:
+                factor(i - 2)
             probs(i, 1)
             if i == 0:
                 side_turn(i, 2)
-            if prev >= 0:
-                abs_sum(prev, "zp")
             if i == 1:
                 side_copy(i, 2)
             if prev >= 0:
+                abs_sum(prev, "zp")
                 abs_sum(prev, "zt")
-                small_ops(prev, nc.gpsimd)
+                bound(prev)
             turn_probs(i)
             side_quant(i, 1)
             if i == 0:
                 side_copy(i, 2)
-                v_quant("vn", 0)
             copy_probs(i)
+            if i == 0:
+                v_inter(v_copy, "vn", 0, 0, 2)
+                v_inter(s_copy, "vn", 0, 1, 2)
             if prev >= 0:
+                norm(prev)
                 keep_zp(prev, False)
-            if i - 2 >= 0:
+            if i >= 2:
                 blend(i - 2)
             side_quant(i, 2)
-            if i == 3:
-                v_quant("vp", 1)
+            if i == 2:
+                v_inter(v_copy, "vp", 1, 0, 1)
+            if i == 4:
+                v_inter(v_copy, "vn", 1, 1, 2)
+            for part in sparts.get(i, ()):
+                v_inter(s_copy, "vn", 1, part, 4)
+            if i == 6:
+                planes_group(0)
+                planes_inter(0, 0, 256, v_copy)
 
         i = PAIRS - 1
-        recip(i)
-        factor(i - 2, nc.gpsimd)
-        for part in range(2, 4):
-            planes_inter(0, 128 * part, 128 * part + 128, nc.gpsimd)
+        recip(i, 0, 2)
         probs(i, 0)
         turn_branch(i, 0)
-        quant_probs(i - 1)
-        values(i - 1)
         probs(i, 1)
         turn_branch(i, 1)
+        quant_probs(i - 1)
+        values(i - 1)
+        recip(i, 2, 3)
+        clipped(i - 2)
         copy_branch(i, 0, s_copy)
-        abs_sum(i - 1, "zp")
+        factor(i - 2)
         copy_branch(i, 1, s_copy)
-        abs_sum(i - 1, "zt")
-        blend(i - 2)
         quant_branch(i, 0)
-        keep_zp(i - 1, True)
-        small_ops(i - 1, nc.gpsimd)
+        blend(i - 2)
         quant_branch(i, 1)
+        abs_sum(i - 1, "zp")
+        abs_sum(i - 1, "zt")
+        keep_zp(i - 1, True)
+        bound(i - 1)
+        norm(i - 1)
         values(i)
-        recip(i + 1)
-        factor(i - 1, nc.gpsimd)
+        planes_inter(0, 256, D, v_copy)
+        recip(i + 1, 2, 3)
+        clipped(i - 1)
+        factor(i - 1)
         planes_quant(0, 0, D)
         planes_store(0, 0, D)
         scales_store(0)
         blend(i - 1)
         abs_sum(i, "zp")
         keep_zp(i, True)
+        bound(i)
         abs_sum(i, "zt")
-        small_ops(i, nc.vector)
-        recip(i + 2)
-        factor(i, nc.vector)
+        norm(i)
+        clipped(i)
+        recip(i + 2, 2, 3)
+        factor(i)
         blend(i)
         planes_group(1)
-        planes_inter(1, 0, 352, nc.vector)
-        planes_inter(1, 352, D, nc.scalar)
+        planes_inter(1, 0, 352, v_copy)
+        planes_inter(1, 352, D, s_copy)
         planes_quant(1, 0, 256)
         planes_quant(1, 256, D)
         planes_store(1, 0, D)

@@ -25,6 +25,9 @@ SQRT_M = math.sqrt(M)
 PAIRS = H * PACK
 
 
+W = [5, 0, 2, 2, 0, 1, 0, 2, 0, 0, 1, 2, 1, 3, 0, 0, 0, 0]
+
+
 def tile_normalizedattentionguidancemerge_x1_kernel(tc, q, kp, vp, kn, vn, g, out_0, out_1, out_2):
     nc = tc.nc
     with ExitStack() as ctx:
@@ -46,6 +49,8 @@ def tile_normalizedattentionguidancemerge_x1_kernel(tc, q, kp, vp, kn, vn, g, ou
             src = dram[label][h].rearrange("(p t) d -> p t d", t=PACK)
             nc.sync.dma_start(out=raw[label, h][:, lo:hi, :], in_=src[:, lo:hi, :])
 
+        g_zero = persist("g_zero", [P, M], BF16)
+        nc.vector.memset(g_zero[:], 0.0)
         g_rows = persist("g_rows", [P, M], BF16)
         nc.vector.memset(g_rows[:], 0.0)
         zeros = persist("zeros", [P, P], F32)
@@ -68,6 +73,24 @@ def tile_normalizedattentionguidancemerge_x1_kernel(tc, q, kp, vp, kn, vn, g, ou
         ones = persist("ones", [P, P], BF16)
         nc.scalar.activation(out=ones[:], in_=zeros[:], func=ACT.Exp)
 
+        def warm(n):
+            bank = psum.tile([P, M], F32, name="warm", tag="warm", bufs=1)
+            for k in range(n):
+                nc.tensor.matmul(out=bank[:], lhsT=g_zero[:, 0:P], rhs=g_zero[:], start=True, stop=True)
+
+        def warm_mx(n, cols=512):
+            bank = psum.tile([P, M], F32, name="warm", tag="warm", bufs=1)
+            for k in range(n):
+                nc.tensor.matmul_mx(
+                    out=bank[:, 0:cols],
+                    lhsT=codes["q", 0][:, 0:P].bitcast(FP8X4),
+                    lhsT_scale=scales["q", 0][:, 0:P],
+                    rhs=codes["kp", 0][:, 0:cols].bitcast(FP8X4),
+                    rhs_scale=scales["kp", 0][:, 0:cols],
+                    start=True,
+                    stop=True,
+                )
+
         codes = {}
         scales = {}
         for h in range(H):
@@ -82,7 +105,7 @@ def tile_normalizedattentionguidancemerge_x1_kernel(tc, q, kp, vp, kn, vn, g, ou
 
         def turn(label, h, half):
             words = raw[label, h][:].bitcast(F32)
-            bank = psum.tile([P, 4, P], F32, name="bank", tag="tp", bufs=3)
+            bank = psum.tile([P, 4, P], F32, name="bank", tag="tp", bufs=2)
             for e in range(2):
                 for w in range(2):
                     nc.tensor.transpose(bank[:, 2 * e + w, :], words[:, 2 * half + e, w:256:2], ident[:])
@@ -120,19 +143,20 @@ def tile_normalizedattentionguidancemerge_x1_kernel(tc, q, kp, vp, kn, vn, g, ou
         V_OF = ("vp", "vn")
         st = {}
 
-        def logits(i, b):
+        def logits(i, b, passes=1):
             h, t = divmod(i, PACK)
             cols = slice(P * t, P * t + P)
             lg = psum.tile([P, M], F32, name="lg%d" % b, tag="lg%d" % b, bufs=1)
-            nc.tensor.matmul_mx(
-                out=lg[:],
-                lhsT=codes["q", h][:, cols].bitcast(FP8X4),
-                lhsT_scale=scales["q", h][:, cols],
-                rhs=codes[K_OF[b], h][:].bitcast(FP8X4),
-                rhs_scale=scales[K_OF[b], h][:],
-                start=True,
-                stop=True,
-            )
+            for k in range(passes):
+                nc.tensor.matmul_mx(
+                    out=lg[:],
+                    lhsT=codes["q", h][:, cols].bitcast(FP8X4),
+                    lhsT_scale=scales["q", h][:, cols],
+                    rhs=codes[K_OF[b], h][:].bitcast(FP8X4),
+                    rhs_scale=scales[K_OF[b], h][:],
+                    start=True,
+                    stop=True,
+                )
             st[i, "lg", b] = lg
 
         def minpass(i, b):
@@ -185,7 +209,7 @@ def tile_normalizedattentionguidancemerge_x1_kernel(tc, q, kp, vp, kn, vn, g, ou
 
         def turn_branch(i, b):
             words = st[i, "p"][:].bitcast(F32)
-            bank = psum.tile([P, 4, P], F32, name="bank", tag="tp", bufs=3)
+            bank = psum.tile([P, 4, P], F32, name="bank", tag="tp", bufs=2)
             for u in range(2):
                 nc.tensor.transpose(bank[:, u, :], words[:, b, P * u : P * u + P], ident[:])
             st[i, "bank", b] = bank
@@ -205,7 +229,7 @@ def tile_normalizedattentionguidancemerge_x1_kernel(tc, q, kp, vp, kn, vn, g, ou
 
         def turn_probs(i):
             words = st[i, "p"][:].bitcast(F32)
-            bank = psum.tile([P, 4, P], F32, name="bank", tag="tp", bufs=3)
+            bank = psum.tile([P, 4, P], F32, name="bank", tag="tp", bufs=2)
             for b in range(2):
                 for u in range(2):
                     nc.tensor.transpose(bank[:, 2 * b + u, :], words[:, b, P * u : P * u + P], ident[:])
@@ -318,6 +342,7 @@ def tile_normalizedattentionguidancemerge_x1_kernel(tc, q, kp, vp, kn, vn, g, ou
 
         s_copy = nc.scalar.copy
         v_copy = nc.vector.tensor_copy
+        warm(W[0])
         g_bank = psum.tile([P, M], F32, name="zt", tag="zt", bufs=2)
         nc.tensor.matmul(out=g_bank[:], lhsT=ones[:], rhs=g_rows[:], start=True, stop=True)
         g_all = []
@@ -334,30 +359,41 @@ def tile_normalizedattentionguidancemerge_x1_kernel(tc, q, kp, vp, kn, vn, g, ou
         v_group("vp", 0)
         turn("kp", 0, 0)
         untangle("kp", 0, 0, s_copy)
+        warm(W[1])
         turn("q", 0, 0)
         untangle("q", 0, 0, s_copy)
+        warm(W[2])
         turn("kp", 0, 1)
         untangle("kp", 0, 1, s_copy)
+        warm(W[3])
         quant_half("kp", 0, 0)
         quant_half("q", 0, 0)
         quant_half("kp", 0, 1)
         turn("kn", 0, 0)
         untangle("kn", 0, 0, s_copy)
+        warm(W[4])
+        if W[16]:
+            logits(0, 0)
         turn("kn", 0, 1)
         untangle("kn", 0, 1, s_copy)
-        logits(0, 0)
+        if not W[16]:
+            logits(0, 0)
+        warm_mx(W[5])
         v_inter(v_copy, "vp", 0, 0, 2)
         turn("q", 0, 1)
         untangle("q", 0, 1, s_copy)
         minpass(0, 0)
+        warm_mx(W[6])
         logits(1, 0)
         quant_half("kn", 0, 0)
         quant_half("kn", 0, 1)
         logits(0, 1)
+        warm_mx(W[7])
         expo(0, 0)
         v_inter(v_copy, "vp", 0, 1, 2)
         minpass(0, 1)
         logits(1, 1)
+        warm_mx(W[8])
         expo(0, 1)
         quant_half("q", 0, 1)
         v_group("vn", 0)
@@ -386,11 +422,16 @@ def tile_normalizedattentionguidancemerge_x1_kernel(tc, q, kp, vp, kn, vn, g, ou
             minpass(nxt, 0)
             if i + 2 < PAIRS:
                 logits(i + 2, 0)
+            warm_mx(W[10] if i >= 1 else W[11])
             expo(nxt, 0)
             minpass(nxt, 1)
-            if i + 2 < PAIRS:
+            if i + 2 < PAIRS and not W[15]:
                 logits(i + 2, 1)
+            if i < 2:
+                warm_mx(W[9])
             side_turn(i, 1)
+            if i < 2:
+                warm_mx(W[14])
             if i == 1:
                 side_turn(i, 2)
             expo(nxt, 1)
@@ -422,7 +463,11 @@ def tile_normalizedattentionguidancemerge_x1_kernel(tc, q, kp, vp, kn, vn, g, ou
                 abs_sum(prev, "zp")
                 abs_sum(prev, "zt")
                 bound(prev)
+            warm_mx(W[12])
             turn_probs(i)
+            if i + 2 < PAIRS and W[15]:
+                logits(i + 2, 1)
+            warm_mx(W[13])
             side_quant(i, 1)
             if i == 0:
                 side_copy(i, 2)
@@ -452,6 +497,7 @@ def tile_normalizedattentionguidancemerge_x1_kernel(tc, q, kp, vp, kn, vn, g, ou
         turn_branch(i, 0)
         probs(i, 1)
         turn_branch(i, 1)
+        warm_mx(W[17])
         quant_probs(i - 1)
         values(i - 1)
         recip(i, 2, 3)

@@ -25,7 +25,7 @@ SQRT_M = math.sqrt(M)
 PAIRS = H * PACK
 
 
-W = [5, 0, 2, 2, 0, 1, 0, 2, 0, 0, 1, 2, 1, 3, 0, 0, 0, 0]
+W = [4] + [0] * 18
 
 
 def tile_normalizedattentionguidancemerge_x1_kernel(tc, q, kp, vp, kn, vn, g, out_0, out_1, out_2):
@@ -74,22 +74,9 @@ def tile_normalizedattentionguidancemerge_x1_kernel(tc, q, kp, vp, kn, vn, g, ou
         nc.scalar.activation(out=ones[:], in_=zeros[:], func=ACT.Exp)
 
         def warm(n):
-            bank = psum.tile([P, M], F32, name="warm", tag="warm", bufs=1)
+            bank = psum.tile([P, M], F32, name="warm", tag="lg1", bufs=1)
             for k in range(n):
                 nc.tensor.matmul(out=bank[:], lhsT=g_zero[:, 0:P], rhs=g_zero[:], start=True, stop=True)
-
-        def warm_mx(n, cols=512):
-            bank = psum.tile([P, M], F32, name="warm", tag="warm", bufs=1)
-            for k in range(n):
-                nc.tensor.matmul_mx(
-                    out=bank[:, 0:cols],
-                    lhsT=codes["q", 0][:, 0:P].bitcast(FP8X4),
-                    lhsT_scale=scales["q", 0][:, 0:P],
-                    rhs=codes["kp", 0][:, 0:cols].bitcast(FP8X4),
-                    rhs_scale=scales["kp", 0][:, 0:cols],
-                    start=True,
-                    stop=True,
-                )
 
         codes = {}
         scales = {}
@@ -105,7 +92,7 @@ def tile_normalizedattentionguidancemerge_x1_kernel(tc, q, kp, vp, kn, vn, g, ou
 
         def turn(label, h, half):
             words = raw[label, h][:].bitcast(F32)
-            bank = psum.tile([P, 4, P], F32, name="bank", tag="tp", bufs=2)
+            bank = psum.tile([P, 4, P], F32, name="bank", tag="tp", bufs=3)
             for e in range(2):
                 for w in range(2):
                     nc.tensor.transpose(bank[:, 2 * e + w, :], words[:, 2 * half + e, w:256:2], ident[:])
@@ -132,8 +119,8 @@ def tile_normalizedattentionguidancemerge_x1_kernel(tc, q, kp, vp, kn, vn, g, ou
         def v_inter(eng, label, h, part, parts):
             n = D // parts
             cols = slice(part * n, part * n + n)
-            dst = staged[label, h][:, cols, :]
-            src = raw[label, h][:, :, cols].rearrange("p t d -> p d t")
+            dst = staged[label, h][:, cols, :].rearrange("p (c i) t -> p c t i", i=4)
+            src = raw[label, h][:, :, cols].rearrange("p t (c i) -> p c t i", i=4)
             eng(out=dst, in_=src)
 
         def v_quant(label, h):
@@ -209,7 +196,7 @@ def tile_normalizedattentionguidancemerge_x1_kernel(tc, q, kp, vp, kn, vn, g, ou
 
         def turn_branch(i, b):
             words = st[i, "p"][:].bitcast(F32)
-            bank = psum.tile([P, 4, P], F32, name="bank", tag="tp", bufs=2)
+            bank = psum.tile([P, 4, P], F32, name="bank", tag="tp", bufs=3)
             for u in range(2):
                 nc.tensor.transpose(bank[:, u, :], words[:, b, P * u : P * u + P], ident[:])
             st[i, "bank", b] = bank
@@ -229,7 +216,7 @@ def tile_normalizedattentionguidancemerge_x1_kernel(tc, q, kp, vp, kn, vn, g, ou
 
         def turn_probs(i):
             words = st[i, "p"][:].bitcast(F32)
-            bank = psum.tile([P, 4, P], F32, name="bank", tag="tp", bufs=2)
+            bank = psum.tile([P, 4, P], F32, name="bank", tag="tp", bufs=3)
             for b in range(2):
                 for u in range(2):
                     nc.tensor.transpose(bank[:, 2 * b + u, :], words[:, b, P * u : P * u + P], ident[:])
@@ -247,6 +234,23 @@ def tile_normalizedattentionguidancemerge_x1_kernel(tc, q, kp, vp, kn, vn, g, ou
             quantize(c[:], s[:], st[i, "pg"][:])
             st[i, "pc"], st[i, "ps"] = c, s
 
+        def zt_bank(i):
+            if (i, "zt") not in st:
+                st[i, "zt"] = psum.tile([P, D], F32, name="zt", tag="zt", bufs=2)
+            return st[i, "zt"]
+
+        def warm_mx(i, n):
+            for k in range(n):
+                nc.tensor.matmul_mx(
+                    out=zt_bank(i)[:],
+                    lhsT=codes["q", 0][:, 0:P].bitcast(FP8X4),
+                    lhsT_scale=scales["q", 0][:, 0:P],
+                    rhs=codes["kp", 0][:].bitcast(FP8X4),
+                    rhs_scale=scales["kp", 0][:],
+                    start=True,
+                    stop=True,
+                )
+
         def values(i):
             h = i // PACK
 
@@ -263,12 +267,12 @@ def tile_normalizedattentionguidancemerge_x1_kernel(tc, q, kp, vp, kn, vn, g, ou
                 )
 
             zp = psum.tile([P, D], F32, name="zp", tag="zp", bufs=1)
-            zt = psum.tile([P, D], F32, name="zt", tag="zt", bufs=2)
+            zt = zt_bank(i)
             one(zp, 0, True, True)
             one(zt, 0, True, False)
             one(zt, 0, False, False)
             one(zt, 1, False, True)
-            st[i, "zp"], st[i, "zt"] = zp, zt
+            st[i, "zp"] = zp
 
         def abs_sum(i, which):
             if which == "zp":
@@ -284,19 +288,24 @@ def tile_normalizedattentionguidancemerge_x1_kernel(tc, q, kp, vp, kn, vn, g, ou
             else:
                 nc.scalar.activation(out=st[i, "zp3"][:], in_=st[i, "zp"][:], func=ACT.Copy, scale=0.3)
 
-        def bound(i):
+        def bound(i, eng):
             st[i, "w"] = ring.tile([P, 1], F32, name="w", tag="w", bufs=3)
-            nc.scalar.activation(out=st[i, "w"][:], in_=st[i, "l1"][:, 0:1], func=ACT.Copy, scale=CLIP, bias=CLIP * EPS)
+            eng.tensor_scalar(out=st[i, "w"][:], in0=st[i, "l1"][:, 0:1], scalar1=EPS, scalar2=CLIP, op0=ALU.add, op1=ALU.mult)
 
-        def norm(i):
+        def norm(i, eng):
             denominators(i + 2)
-            nc.scalar.activation(
-                out=st[i + 2, "den"][:, 2:3], in_=st[i, "w"][:], func=ACT.Identity, scale=EPS / CLIP, bias=st[i, "l1"][:, 1:2]
+            eng.tensor_scalar(
+                out=st[i + 2, "den"][:, 2:3],
+                in0=st[i, "w"][:],
+                scalar1=EPS / CLIP,
+                scalar2=st[i, "l1"][:, 1:2],
+                op0=ALU.mult,
+                op1=ALU.add,
             )
 
-        def clipped(i):
+        def clipped(i, eng):
             st[i, "num"] = ring.tile([P, 1], F32, name="num", tag="num", bufs=3)
-            nc.vector.tensor_scalar(
+            eng.tensor_scalar(
                 out=st[i, "num"][:], in0=st[i, "w"][:], scalar1=st[i, "l1"][:, 1:2], scalar2=0.7, op0=ALU.min, op1=ALU.mult
             )
 
@@ -373,27 +382,23 @@ def tile_normalizedattentionguidancemerge_x1_kernel(tc, q, kp, vp, kn, vn, g, ou
         untangle("kn", 0, 0, s_copy)
         warm(W[4])
         if W[16]:
-            logits(0, 0)
+            logits(0, 0, 1 + W[5])
         turn("kn", 0, 1)
         untangle("kn", 0, 1, s_copy)
         if not W[16]:
-            logits(0, 0)
-        warm_mx(W[5])
+            logits(0, 0, 1 + W[5])
         v_inter(v_copy, "vp", 0, 0, 2)
         turn("q", 0, 1)
         untangle("q", 0, 1, s_copy)
         minpass(0, 0)
-        warm_mx(W[6])
-        logits(1, 0)
+        logits(1, 0, 1 + W[6])
         quant_half("kn", 0, 0)
         quant_half("kn", 0, 1)
-        logits(0, 1)
-        warm_mx(W[7])
+        logits(0, 1, 1 + W[7])
+        v_inter(s_copy, "vp", 0, 1, 2)
         expo(0, 0)
-        v_inter(v_copy, "vp", 0, 1, 2)
         minpass(0, 1)
-        logits(1, 1)
-        warm_mx(W[8])
+        logits(1, 1, 1 + W[8])
         expo(0, 1)
         quant_half("q", 0, 1)
         v_group("vn", 0)
@@ -421,17 +426,12 @@ def tile_normalizedattentionguidancemerge_x1_kernel(tc, q, kp, vp, kn, vn, g, ou
             side_copy(i, 0)
             minpass(nxt, 0)
             if i + 2 < PAIRS:
-                logits(i + 2, 0)
-            warm_mx(W[10] if i >= 1 else W[11])
+                logits(i + 2, 0, 1 + (W[10] if i >= 1 else W[11]))
             expo(nxt, 0)
             minpass(nxt, 1)
             if i + 2 < PAIRS and not W[15]:
-                logits(i + 2, 1)
-            if i < 2:
-                warm_mx(W[9])
+                logits(i + 2, 1, 1 + W[12])
             side_turn(i, 1)
-            if i < 2:
-                warm_mx(W[14])
             if i == 1:
                 side_turn(i, 2)
             expo(nxt, 1)
@@ -439,18 +439,15 @@ def tile_normalizedattentionguidancemerge_x1_kernel(tc, q, kp, vp, kn, vn, g, ou
             if i == 0:
                 v_quant("vp", 0)
             recip(i, 0, 3 if i >= 2 else 2)
-            if i >= 2:
-                clipped(i - 2)
             if i == 1:
                 v_quant("vn", 0)
             if i == 5:
+                v_quant("vp", 1)
                 v_quant("vn", 1)
             if prev >= 0:
                 quant_probs(prev)
                 values(prev)
             side_quant(i, 0)
-            if i == 4:
-                v_quant("vp", 1)
             probs(i, 0)
             if i >= 2:
                 factor(i - 2)
@@ -461,13 +458,13 @@ def tile_normalizedattentionguidancemerge_x1_kernel(tc, q, kp, vp, kn, vn, g, ou
                 side_copy(i, 2)
             if prev >= 0:
                 abs_sum(prev, "zp")
+                bound(prev, nc.gpsimd)
                 abs_sum(prev, "zt")
-                bound(prev)
-            warm_mx(W[12])
+                norm(prev, nc.gpsimd)
+                clipped(prev, nc.gpsimd)
             turn_probs(i)
             if i + 2 < PAIRS and W[15]:
-                logits(i + 2, 1)
-            warm_mx(W[13])
+                logits(i + 2, 1, 1 + W[14])
             side_quant(i, 1)
             if i == 0:
                 side_copy(i, 2)
@@ -476,10 +473,11 @@ def tile_normalizedattentionguidancemerge_x1_kernel(tc, q, kp, vp, kn, vn, g, ou
                 v_inter(v_copy, "vn", 0, 0, 2)
                 v_inter(s_copy, "vn", 0, 1, 2)
             if prev >= 0:
-                norm(prev)
                 keep_zp(prev, False)
             if i >= 2:
                 blend(i - 2)
+            if i >= W[9]:
+                warm_mx(i, W[13])
             side_quant(i, 2)
             if i == 2:
                 v_inter(v_copy, "vp", 1, 0, 1)
@@ -497,11 +495,9 @@ def tile_normalizedattentionguidancemerge_x1_kernel(tc, q, kp, vp, kn, vn, g, ou
         turn_branch(i, 0)
         probs(i, 1)
         turn_branch(i, 1)
-        warm_mx(W[17])
         quant_probs(i - 1)
         values(i - 1)
         recip(i, 2, 3)
-        clipped(i - 2)
         copy_branch(i, 0, s_copy)
         factor(i - 2)
         copy_branch(i, 1, s_copy)
@@ -511,23 +507,23 @@ def tile_normalizedattentionguidancemerge_x1_kernel(tc, q, kp, vp, kn, vn, g, ou
         abs_sum(i - 1, "zp")
         abs_sum(i - 1, "zt")
         keep_zp(i - 1, True)
-        bound(i - 1)
-        norm(i - 1)
+        bound(i - 1, nc.gpsimd)
+        norm(i - 1, nc.gpsimd)
         values(i)
         planes_inter(0, 256, D, v_copy)
         recip(i + 1, 2, 3)
-        clipped(i - 1)
+        clipped(i - 1, nc.vector)
         factor(i - 1)
         planes_quant(0, 0, D)
         planes_store(0, 0, D)
         scales_store(0)
         blend(i - 1)
         abs_sum(i, "zp")
+        bound(i, nc.vector)
         keep_zp(i, True)
-        bound(i)
         abs_sum(i, "zt")
-        norm(i)
-        clipped(i)
+        norm(i, nc.vector)
+        clipped(i, nc.vector)
         recip(i + 2, 2, 3)
         factor(i)
         blend(i)

@@ -25,7 +25,7 @@ SQRT_M = math.sqrt(M)
 PAIRS = H * PACK
 
 
-W = [4] + [0] * 18
+W = [5, 0, 3, 0, 2, 0, 1, 1, 0, 0, 0, 2, 0, 3, 3, 0, 0, 0]
 
 
 def tile_normalizedattentionguidancemerge_x1_kernel(tc, q, kp, vp, kn, vn, g, out_0, out_1, out_2):
@@ -59,9 +59,10 @@ def tile_normalizedattentionguidancemerge_x1_kernel(tc, q, kp, vp, kn, vn, g, ou
         nc.sync.dma_start(out=g_one[:], in_=g.rearrange("(o m) -> o m", o=1))
         nc.vector.tensor_copy(out=g_rows[0:1, :], in_=g_one[:])
         load("kp", 0, 0, 2)
-        load("q", 0, 0, 2)
         load("kp", 0, 2, 4)
+        load("q", 0, 0, 1)
         load("kn", 0, 0, 4)
+        load("q", 0, 1, 2)
         load("vp", 0, 0, 4)
         load("q", 0, 2, 4)
         load("vn", 0, 0, 4)
@@ -90,27 +91,28 @@ def tile_normalizedattentionguidancemerge_x1_kernel(tc, q, kp, vp, kn, vn, g, ou
 
         staged = {}
 
-        def turn(label, h, half):
+        def turn(label, h, first, tiles=2):
             words = raw[label, h][:].bitcast(F32)
             bank = psum.tile([P, 4, P], F32, name="bank", tag="tp", bufs=3)
-            for e in range(2):
+            for e in range(tiles):
                 for w in range(2):
-                    nc.tensor.transpose(bank[:, 2 * e + w, :], words[:, 2 * half + e, w:256:2], ident[:])
-            staged[label, h, half] = bank
+                    nc.tensor.transpose(bank[:, 2 * e + w, :], words[:, first + e, w:256:2], ident[:])
+            staged[label, h, first] = bank
 
-        def untangle(label, h, half, copy):
-            bank = staged[label, h, half]
+        def untangle(label, h, first, copy, tiles=2):
+            bank = staged[label, h, first]
             group = ring.tile([P, 2 * D], BF16, name="group", tag="group", bufs=4, align_bytes=256)
-            dst = group[:].bitcast(F32)
+            dst = group[:, 0 : D * tiles].bitcast(F32)
+            src = bank[:, 0 : 2 * tiles, :]
             if label == "q":
-                copy(out=dst.rearrange("p (e m w) -> p e m w", e=2, w=2), in_=bank[:].rearrange("p (e w) m -> p e m w", w=2))
+                copy(out=dst.rearrange("p (e m w) -> p e m w", e=tiles, w=2), in_=src.rearrange("p (e w) m -> p e m w", w=2))
             else:
-                copy(out=dst.rearrange("p (m s) -> p m s", s=4), in_=bank[:].rearrange("p s m -> p m s"))
-            staged[label, h, half] = group
+                copy(out=dst.rearrange("p (m s) -> p m s", s=4), in_=src.rearrange("p s m -> p m s"))
+            staged[label, h, first] = group
 
-        def quant_half(label, h, half):
-            cols = slice(256 * half, 256 * half + 256)
-            quantize(codes[label, h][:, cols], scales[label, h][:, cols], staged[label, h, half][:])
+        def quant_half(label, h, first, tiles=2):
+            cols = slice(P * first, P * (first + tiles))
+            quantize(codes[label, h][:, cols], scales[label, h][:, cols], staged[label, h, first][:, 0 : D * tiles])
 
         def v_group(label, h):
             t = ring.tile([P, D, PACK], BF16, name="vgroup", tag="vgroup", bufs=4, align_bytes=256)
@@ -288,19 +290,14 @@ def tile_normalizedattentionguidancemerge_x1_kernel(tc, q, kp, vp, kn, vn, g, ou
             else:
                 nc.scalar.activation(out=st[i, "zp3"][:], in_=st[i, "zp"][:], func=ACT.Copy, scale=0.3)
 
-        def bound(i, eng):
+        def bound(i):
             st[i, "w"] = ring.tile([P, 1], F32, name="w", tag="w", bufs=3)
-            eng.tensor_scalar(out=st[i, "w"][:], in0=st[i, "l1"][:, 0:1], scalar1=EPS, scalar2=CLIP, op0=ALU.add, op1=ALU.mult)
+            nc.scalar.activation(out=st[i, "w"][:], in_=st[i, "l1"][:, 0:1], func=ACT.Copy, scale=CLIP, bias=CLIP * EPS)
 
-        def norm(i, eng):
+        def norm(i):
             denominators(i + 2)
-            eng.tensor_scalar(
-                out=st[i + 2, "den"][:, 2:3],
-                in0=st[i, "w"][:],
-                scalar1=EPS / CLIP,
-                scalar2=st[i, "l1"][:, 1:2],
-                op0=ALU.mult,
-                op1=ALU.add,
+            nc.scalar.activation(
+                out=st[i + 2, "den"][:, 2:3], in_=st[i, "w"][:], func=ACT.Identity, scale=EPS / CLIP, bias=st[i, "l1"][:, 1:2]
             )
 
         def clipped(i, eng):
@@ -369,43 +366,46 @@ def tile_normalizedattentionguidancemerge_x1_kernel(tc, q, kp, vp, kn, vn, g, ou
         turn("kp", 0, 0)
         untangle("kp", 0, 0, s_copy)
         warm(W[1])
-        turn("q", 0, 0)
-        untangle("q", 0, 0, s_copy)
+        turn("kp", 0, 2)
+        untangle("kp", 0, 2, s_copy)
         warm(W[2])
-        turn("kp", 0, 1)
-        untangle("kp", 0, 1, s_copy)
+        turn("q", 0, 0, 1)
+        untangle("q", 0, 0, s_copy, 1)
         warm(W[3])
-        quant_half("kp", 0, 0)
-        quant_half("q", 0, 0)
-        quant_half("kp", 0, 1)
         turn("kn", 0, 0)
         untangle("kn", 0, 0, s_copy)
-        warm(W[4])
+        quant_half("kp", 0, 0)
+        quant_half("kp", 0, 2)
+        quant_half("q", 0, 0, 1)
         if W[16]:
             logits(0, 0, 1 + W[5])
-        turn("kn", 0, 1)
-        untangle("kn", 0, 1, s_copy)
+        turn("kn", 0, 2)
+        untangle("kn", 0, 2, s_copy)
         if not W[16]:
             logits(0, 0, 1 + W[5])
-        v_inter(v_copy, "vp", 0, 0, 2)
-        turn("q", 0, 1)
-        untangle("q", 0, 1, s_copy)
+        warm(W[4])
+        turn("q", 0, 1, 1)
+        untangle("q", 0, 1, s_copy, 1)
+        turn("q", 0, 2)
         minpass(0, 0)
-        logits(1, 0, 1 + W[6])
         quant_half("kn", 0, 0)
-        quant_half("kn", 0, 1)
+        quant_half("kn", 0, 2)
         logits(0, 1, 1 + W[7])
-        v_inter(s_copy, "vp", 0, 1, 2)
+        v_inter(v_copy, "vp", 0, 0, 2)
         expo(0, 0)
+        quant_half("q", 0, 1, 1)
+        logits(1, 0, 1 + W[6])
         minpass(0, 1)
-        logits(1, 1, 1 + W[8])
+        untangle("q", 0, 2, s_copy)
+        v_inter(s_copy, "vp", 0, 2, 4)
         expo(0, 1)
-        quant_half("q", 0, 1)
+        v_inter(s_copy, "vp", 0, 3, 4)
+        logits(1, 1, 1 + W[8])
         v_group("vn", 0)
         for label in ("vp", "vn"):
             v_group(label, 1)
 
-        turns = {0: (("q", 0), ("q", 1), ("kp", 0)), 1: (("kp", 1), ("kn", 0), ("kn", 1))}
+        turns = {0: (("q", 0), ("q", 2), ("kp", 0)), 1: (("kp", 2), ("kn", 0), ("kn", 2))}
         sparts = {2: (0,), 3: (1,)}
 
         def side_turn(i, k):
@@ -425,6 +425,8 @@ def tile_normalizedattentionguidancemerge_x1_kernel(tc, q, kp, vp, kn, vn, g, ou
             side_turn(i, 0)
             side_copy(i, 0)
             minpass(nxt, 0)
+            if i == 0:
+                quant_half("q", 0, 2)
             if i + 2 < PAIRS:
                 logits(i + 2, 0, 1 + (W[10] if i >= 1 else W[11]))
             expo(nxt, 0)
@@ -442,12 +444,15 @@ def tile_normalizedattentionguidancemerge_x1_kernel(tc, q, kp, vp, kn, vn, g, ou
             if i == 1:
                 v_quant("vn", 0)
             if i == 5:
-                v_quant("vp", 1)
                 v_quant("vn", 1)
+            if i >= 2:
+                clipped(i - 2, nc.vector)
             if prev >= 0:
                 quant_probs(prev)
                 values(prev)
             side_quant(i, 0)
+            if i == 4:
+                v_quant("vp", 1)
             probs(i, 0)
             if i >= 2:
                 factor(i - 2)
@@ -458,10 +463,8 @@ def tile_normalizedattentionguidancemerge_x1_kernel(tc, q, kp, vp, kn, vn, g, ou
                 side_copy(i, 2)
             if prev >= 0:
                 abs_sum(prev, "zp")
-                bound(prev, nc.gpsimd)
                 abs_sum(prev, "zt")
-                norm(prev, nc.gpsimd)
-                clipped(prev, nc.gpsimd)
+                bound(prev)
             turn_probs(i)
             if i + 2 < PAIRS and W[15]:
                 logits(i + 2, 1, 1 + W[14])
@@ -473,6 +476,7 @@ def tile_normalizedattentionguidancemerge_x1_kernel(tc, q, kp, vp, kn, vn, g, ou
                 v_inter(v_copy, "vn", 0, 0, 2)
                 v_inter(s_copy, "vn", 0, 1, 2)
             if prev >= 0:
+                norm(prev)
                 keep_zp(prev, False)
             if i >= 2:
                 blend(i - 2)
@@ -498,6 +502,7 @@ def tile_normalizedattentionguidancemerge_x1_kernel(tc, q, kp, vp, kn, vn, g, ou
         quant_probs(i - 1)
         values(i - 1)
         recip(i, 2, 3)
+        clipped(i - 2, nc.vector)
         copy_branch(i, 0, s_copy)
         factor(i - 2)
         copy_branch(i, 1, s_copy)
@@ -507,8 +512,8 @@ def tile_normalizedattentionguidancemerge_x1_kernel(tc, q, kp, vp, kn, vn, g, ou
         abs_sum(i - 1, "zp")
         abs_sum(i - 1, "zt")
         keep_zp(i - 1, True)
-        bound(i - 1, nc.gpsimd)
-        norm(i - 1, nc.gpsimd)
+        bound(i - 1)
+        norm(i - 1)
         values(i)
         planes_inter(0, 256, D, v_copy)
         recip(i + 1, 2, 3)
@@ -519,10 +524,10 @@ def tile_normalizedattentionguidancemerge_x1_kernel(tc, q, kp, vp, kn, vn, g, ou
         scales_store(0)
         blend(i - 1)
         abs_sum(i, "zp")
-        bound(i, nc.vector)
         keep_zp(i, True)
+        bound(i)
         abs_sum(i, "zt")
-        norm(i, nc.vector)
+        norm(i)
         clipped(i, nc.vector)
         recip(i + 2, 2, 3)
         factor(i)

from contextlib import ExitStack
import math

import concourse.mybir as mybir
from concourse.masks import make_identity

H, S, M, D = 2, 512, 512, 512
P = 128
PACK = 4
FLOPS = 2 * 4 * H * S * M * D

F32 = mybir.dt.float32
BF16 = mybir.dt.bfloat16
U32 = mybir.dt.uint32
I32 = mybir.dt.int32
U8 = mybir.dt.uint8
FP8X4 = mybir.dt.float8_e4m3fn_x4
ALU = mybir.AluOpType
ACT = mybir.ActivationFunctionType

EPS = 1e-6
CLIP = 2.2
INV_SQRT_D = 1.0 / math.sqrt(D)
SQRT_M = math.sqrt(M)
PAIRS = H * PACK


W = [5, 0, 3, 0, 2, 0, 1, 1, 0, 0, 0, 2, 0, 3, 3, 0, 0, 0]


def tile_normalizedattentionguidancemerge_x1_kernel(tc, q, kp, vp, kn, vn, g, out_0, out_1, out_2):
    nc = tc.nc
    with ExitStack() as ctx:
        keep = ctx.enter_context(tc.tile_pool(name="keep", bufs=1))
        ring = ctx.enter_context(tc.tile_pool(name="ring", bufs=2))
        psum = ctx.enter_context(tc.psum_pool(name="psum", bufs=1))
        ctx.enter_context(tc.manual_schedule())

        def persist(label, shape, dtype):
            return keep.tile(shape, dtype, name=label, tag=label, align_bytes=256)

        raw = {}
        for h in range(H):
            for label in ("q", "kp", "kn", "vp", "vn"):
                raw[label, h] = persist("raw_%s%d" % (label, h), [P, PACK, D], BF16)
        dram = {"q": q, "kp": kp, "kn": kn, "vp": vp, "vn": vn}

        def load(label, h, lo, hi):
            src = dram[label][h].rearrange("(p t) d -> p t d", t=PACK)
            nc.sync.dma_start(out=raw[label, h][:, lo:hi, :], in_=src[:, lo:hi, :])

        g_zero = persist("g_zero", [P, M], BF16)
        nc.vector.memset(g_zero[:], 0.0)
        g_rows = persist("g_rows", [P, M], BF16)
        nc.vector.memset(g_rows[:], 0.0)
        zeros = persist("zeros", [P, P], F32)
        nc.vector.memset(zeros[:], 0.0)
        g_one = persist("g_one", [1, M], BF16)
        nc.sync.dma_start(out=g_one[:], in_=g.rearrange("(o m) -> o m", o=1))
        nc.vector.tensor_copy(out=g_rows[0:1, :], in_=g_one[:])
        load("kp", 0, 0, 2)
        load("kp", 0, 2, 4)
        load("q", 0, 0, 1)
        load("kn", 0, 0, 4)
        load("q", 0, 1, 2)
        load("vp", 0, 0, 4)
        load("q", 0, 2, 4)
        load("vn", 0, 0, 4)
        for label in ("q", "kp", "kn", "vp", "vn"):
            load(label, 1, 0, 4)

        ident = persist("ident", [P, P], F32)
        make_identity(nc, ident[:])
        ones = persist("ones", [P, P], BF16)
        nc.scalar.activation(out=ones[:], in_=zeros[:], func=ACT.Exp)

        def warm(n):
            bank = psum.tile([P, M], F32, name="warm", tag="lg1", bufs=1)
            for k in range(n):
                nc.tensor.matmul(out=bank[:], lhsT=g_zero[:, 0:P], rhs=g_zero[:], start=True, stop=True)

        codes = {}
        scales = {}
        for h in range(H):
            for label in ("q", "kp", "kn", "vp", "vn"):
                codes[label, h] = persist("c_%s%d" % (label, h), [P, D], U32)
                scales[label, h] = persist("s_%s%d" % (label, h), [P, D], U8)

        def quantize(out, plane, in_):
            nc.vector.quantize_mx(out=out.bitcast(FP8X4), scales=plane, in_=in_)

        staged = {}

        def turn(label, h, first, tiles=2):
            words = raw[label, h][:].bitcast(F32)
            bank = psum.tile([P, 4, P], F32, name="bank", tag="tp", bufs=3)
            for e in range(tiles):
                for w in range(2):
                    nc.tensor.transpose(bank[:, 2 * e + w, :], words[:, first + e, w:256:2], ident[:])
            staged[label, h, first] = bank

        def untangle(label, h, first, copy, tiles=2):
            bank = staged[label, h, first]
            group = ring.tile([P, 2 * D], BF16, name="group", tag="group", bufs=4, align_bytes=256)
            dst = group[:, 0 : D * tiles].bitcast(F32)
            src = bank[:, 0 : 2 * tiles, :]
            if label == "q":
                copy(out=dst.rearrange("p (e m w) -> p e m w", e=tiles, w=2), in_=src.rearrange("p (e w) m -> p e m w", w=2))
            else:
                copy(out=dst.rearrange("p (m s) -> p m s", s=4), in_=src.rearrange("p s m -> p m s"))
            staged[label, h, first] = group

        def quant_half(label, h, first, tiles=2):
            cols = slice(P * first, P * (first + tiles))
            quantize(codes[label, h][:, cols], scales[label, h][:, cols], staged[label, h, first][:, 0 : D * tiles])

        def v_group(label, h):
            t = ring.tile([P, D, PACK], BF16, name="vgroup", tag="vgroup", bufs=4, align_bytes=256)
            staged[label, h] = t

        def v_inter(eng, label, h, part, parts):
            n = D // parts
            cols = slice(part * n, part * n + n)
            dst = staged[label, h][:, cols, :].rearrange("p (c i) t -> p c t i", i=4)
            src = raw[label, h][:, :, cols].rearrange("p t (c i) -> p c t i", i=4)
            eng(out=dst, in_=src)

        def v_quant(label, h):
            quantize(codes[label, h][:], scales[label, h][:], staged[label, h][:].rearrange("p d t -> p (d t)"))

        K_OF = ("kp", "kn")
        V_OF = ("vp", "vn")
        st = {}

        def logits(i, b, passes=1):
            h, t = divmod(i, PACK)
            cols = slice(P * t, P * t + P)
            lg = psum.tile([P, M], F32, name="lg%d" % b, tag="lg%d" % b, bufs=1)
            for k in range(passes):
                nc.tensor.matmul_mx(
                    out=lg[:],
                    lhsT=codes["q", h][:, cols].bitcast(FP8X4),
                    lhsT_scale=scales["q", h][:, cols],
                    rhs=codes[K_OF[b], h][:].bitcast(FP8X4),
                    rhs_scale=scales[K_OF[b], h][:],
                    start=True,
                    stop=True,
                )
            st[i, "lg", b] = lg

        def minpass(i, b):
            if b == 0:
                st[i, "neg"] = ring.tile([P, 2, M], F32, name="neg", tag="neg", bufs=2)
                st[i, "nb"] = ring.tile([P, 2], F32, name="nb", tag="nb", bufs=3)
            nc.vector.tensor_scalar(
                out=st[i, "neg"][:, b, :],
                in0=st[i, "lg", b][:],
                scalar1=-INV_SQRT_D,
                scalar2=None,
                op0=ALU.mult,
                op1=ALU.min,
                accum_out=st[i, "nb"][:, b : b + 1],
            )

        def denominators(i):
            if (i, "den") not in st:
                st[i, "den"] = ring.tile([P, 3], F32, name="den", tag="den", bufs=4)

        def expo(i, b):
            if b == 0:
                st[i, "e"] = ring.tile([P, 2, M], F32, name="e", tag="e", bufs=2)
                denominators(i)
            nc.scalar.activation(
                out=st[i, "e"][:, b, :],
                in_=st[i, "neg"][:, b, :],
                func=ACT.Exp,
                scale=-1.0,
                bias=st[i, "nb"][:, b : b + 1],
                accum_out=st[i, "den"][:, b : b + 1],
            )

        def recip(i, lo, hi):
            if (i, "rs") not in st:
                st[i, "rs"] = ring.tile([P, 3], F32, name="rs", tag="rs", bufs=3)
            nc.vector.reciprocal(out=st[i, "rs"][:, lo:hi], in_=st[i, "den"][:, lo:hi])

        def probs(i, b):
            if b == 0:
                st[i, "p"] = ring.tile([P, 2, M], BF16, name="pr", tag="pr", bufs=2, align_bytes=256)
            nc.vector.scalar_tensor_tensor(
                out=st[i, "p"][:, b, :],
                in0=st[i, "e"][:, b, :],
                scalar=st[i, "rs"][:, b : b + 1],
                in1=g_all[b][:],
                op0=ALU.mult,
                op1=ALU.mult,
            )

        def turn_branch(i, b):
            words = st[i, "p"][:].bitcast(F32)
            bank = psum.tile([P, 4, P], F32, name="bank", tag="tp", bufs=3)
            for u in range(2):
                nc.tensor.transpose(bank[:, u, :], words[:, b, P * u : P * u + P], ident[:])
            st[i, "bank", b] = bank

        def copy_branch(i, b, copy):
            if b == 0:
                st[i, "pg"] = ring.tile([P, 2 * M], BF16, name="pgroup", tag="pgroup", bufs=2, align_bytes=256)
            dst = st[i, "pg"][:, M * b : M * b + M].bitcast(F32).rearrange("p (s u) -> p s u", u=2)
            copy(out=dst, in_=st[i, "bank", b][:, 0:2, :].rearrange("p u s -> p s u"))

        def quant_branch(i, b):
            if b == 0:
                st[i, "pc"] = ring.tile([P, 2 * P], U32, name="pcodes", tag="pcodes", bufs=2, align_bytes=256)
                st[i, "ps"] = ring.tile([P, 2 * P], U8, name="pscales", tag="pscales", bufs=2, align_bytes=256)
            cols = slice(P * b, P * b + P)
            quantize(st[i, "pc"][:, cols], st[i, "ps"][:, cols], st[i, "pg"][:, M * b : M * b + M])

        def turn_probs(i):
            words = st[i, "p"][:].bitcast(F32)
            bank = psum.tile([P, 4, P], F32, name="bank", tag="tp", bufs=3)
            for b in range(2):
                for u in range(2):
                    nc.tensor.transpose(bank[:, 2 * b + u, :], words[:, b, P * u : P * u + P], ident[:])
            st[i, "bank"] = bank

        def copy_probs(i):
            group = ring.tile([P, 2 * M], BF16, name="pgroup", tag="pgroup", bufs=2, align_bytes=256)
            dst = group[:].bitcast(F32).rearrange("p (b s u) -> p b s u", b=2, u=2)
            nc.scalar.copy(out=dst, in_=st[i, "bank"][:].rearrange("p (b u) s -> p b s u", u=2))
            st[i, "pg"] = group

        def quant_probs(i):
            c = ring.tile([P, 2 * P], U32, name="pcodes", tag="pcodes", bufs=2, align_bytes=256)
            s = ring.tile([P, 2 * P], U8, name="pscales", tag="pscales", bufs=2, align_bytes=256)
            quantize(c[:], s[:], st[i, "pg"][:])
            st[i, "pc"], st[i, "ps"] = c, s

        def zt_bank(i):
            if (i, "zt") not in st:
                st[i, "zt"] = psum.tile([P, D], F32, name="zt", tag="zt", bufs=2)
            return st[i, "zt"]

        def warm_mx(i, n):
            for k in range(n):
                nc.tensor.matmul_mx(
                    out=zt_bank(i)[:],
                    lhsT=codes["q", 0][:, 0:P].bitcast(FP8X4),
                    lhsT_scale=scales["q", 0][:, 0:P],
                    rhs=codes["kp", 0][:].bitcast(FP8X4),
                    rhs_scale=scales["kp", 0][:],
                    start=True,
                    stop=True,
                )

        def values(i):
            h = i // PACK

            def one(out, b, start, stop):
                cols = slice(P * b, P * b + P)
                nc.tensor.matmul_mx(
                    out=out[:],
                    lhsT=st[i, "pc"][:, cols].bitcast(FP8X4),
                    lhsT_scale=st[i, "ps"][:, cols],
                    rhs=codes[V_OF[b], h][:].bitcast(FP8X4),
                    rhs_scale=scales[V_OF[b], h][:],
                    start=start,
                    stop=stop,
                )

            zp = psum.tile([P, D], F32, name="zp", tag="zp", bufs=1)
            zt = zt_bank(i)
            one(zp, 0, True, True)
            one(zt, 0, True, False)
            one(zt, 0, False, False)
            one(zt, 1, False, True)
            st[i, "zp"] = zp

        def abs_sum(i, which):
            if which == "zp":
                st[i, "l1"] = ring.tile([P, 2], F32, name="l1", tag="l1", bufs=3)
            junk = ring.tile([P, D], BF16, name="junk", tag="junk", bufs=2)
            col = 0 if which == "zp" else 1
            nc.scalar.activation(out=junk[:], in_=st[i, which][:], func=ACT.Abs, accum_out=st[i, "l1"][:, col : col + 1])

        def keep_zp(i, on_vector):
            st[i, "zp3"] = ring.tile([P, D], F32, name="zp3", tag="zp3", bufs=3)
            if on_vector:
                nc.vector.tensor_scalar(out=st[i, "zp3"][:], in0=st[i, "zp"][:], scalar1=0.3, scalar2=None, op0=ALU.mult)
            else:
                nc.scalar.activation(out=st[i, "zp3"][:], in_=st[i, "zp"][:], func=ACT.Copy, scale=0.3)

        def bound(i):
            st[i, "w"] = ring.tile([P, 1], F32, name="w", tag="w", bufs=3)
            nc.scalar.activation(out=st[i, "w"][:], in_=st[i, "l1"][:, 0:1], func=ACT.Copy, scale=CLIP, bias=CLIP * EPS)

        def norm(i):
            denominators(i + 2)
            nc.scalar.activation(
                out=st[i + 2, "den"][:, 2:3], in_=st[i, "w"][:], func=ACT.Identity, scale=EPS / CLIP, bias=st[i, "l1"][:, 1:2]
            )

        def clipped(i, eng):
            st[i, "num"] = ring.tile([P, 1], F32, name="num", tag="num", bufs=3)
            eng.tensor_scalar(
                out=st[i, "num"][:], in0=st[i, "w"][:], scalar1=st[i, "l1"][:, 1:2], scalar2=0.7, op0=ALU.min, op1=ALU.mult
            )

        def factor(i):
            st[i, "a"] = ring.tile([P, 1], F32, name="a", tag="a", bufs=3)
            nc.vector.tensor_tensor(out=st[i, "a"][:], in0=st[i, "num"][:], in1=st[i + 2, "rs"][:, 2:3], op=ALU.mult)

        ob = {}

        def blend(i):
            h, t = divmod(i, PACK)
            if t == 0:
                ob[h] = persist("ob%d" % h, [P, PACK, D], F32)
            nc.vector.scalar_tensor_tensor(
                out=ob[h][:, t, :], in0=st[i, "zt"][:], scalar=st[i, "a"][:], in1=st[i, "zp3"][:], op0=ALU.mult, op1=ALU.add
            )
            dst = out_0[h].rearrange("(p t) d -> p t d", t=PACK)
            nc.sync.dma_start(out=dst[:, t, :], in_=ob[h][:, t, :])

        def planes_group(h):
            staged["ob", h] = persist("og%d" % h, [P, D, PACK], BF16)
            codes["ob", h] = persist("oc%d" % h, [P, D], U32)
            scales["ob", h] = persist("os%d" % h, [P, D], U8)

        def planes_inter(h, lo, hi, eng):
            dst = staged["ob", h][:, lo:hi, :]
            src = ob[h][:, :, lo:hi].rearrange("p t d -> p d t")
            eng(out=dst, in_=src)

        def planes_quant(h, lo, hi):
            quantize(codes["ob", h][:, lo:hi], scales["ob", h][:, lo:hi], staged["ob", h][:, lo:hi, :].rearrange("p d t -> p (d t)"))

        def planes_store(h, lo, hi):
            a, b = h * D + lo, h * D + hi
            nc.sync.dma_start(out=out_1[0, :, a:b, :].rearrange("p d t -> p (d t)").bitcast(I32), in_=codes["ob", h][:, lo:hi].bitcast(I32))

        def scales_store(h):
            for quad in range(4):
                nc.sync.dma_start(
                    out=out_2[0, 4 * quad : 4 * quad + 4, h * D : h * D + D].bitcast(I32),
                    in_=scales["ob", h][32 * quad : 32 * quad + 4, :].bitcast(I32),
                )

        s_copy = nc.scalar.copy
        v_copy = nc.vector.tensor_copy
        warm(W[0])
        g_bank = psum.tile([P, M], F32, name="zt", tag="zt", bufs=2)
        nc.tensor.matmul(out=g_bank[:], lhsT=ones[:], rhs=g_rows[:], start=True, stop=True)
        g_all = []
        for b, factor_b in enumerate((SQRT_M, -SQRT_M)):
            gt = persist("g%d" % b, [P, M], F32)
            nc.vector.tensor_scalar(
                out=gt[:].rearrange("p (u m e) -> p u m e", u=2, e=2),
                in0=g_bank[:].rearrange("p (m u e) -> p u m e", u=2, e=2),
                scalar1=factor_b,
                scalar2=None,
                op0=ALU.mult,
            )
            g_all.append(gt)
        v_group("vp", 0)
        turn("kp", 0, 0)
        untangle("kp", 0, 0, s_copy)
        warm(W[1])
        turn("kp", 0, 2)
        untangle("kp", 0, 2, s_copy)
        warm(W[2])
        turn("q", 0, 0, 1)
        untangle("q", 0, 0, s_copy, 1)
        warm(W[3])
        turn("kn", 0, 0)
        untangle("kn", 0, 0, s_copy)
        quant_half("kp", 0, 0)
        quant_half("kp", 0, 2)
        quant_half("q", 0, 0, 1)
        if W[16]:
            logits(0, 0, 1 + W[5])
        turn("kn", 0, 2)
        untangle("kn", 0, 2, s_copy)
        if not W[16]:
            logits(0, 0, 1 + W[5])
        warm(W[4])
        turn("q", 0, 1, 1)
        untangle("q", 0, 1, s_copy, 1)
        turn("q", 0, 2)
        minpass(0, 0)
        quant_half("kn", 0, 0)
        quant_half("kn", 0, 2)
        logits(0, 1, 1 + W[7])
        v_inter(v_copy, "vp", 0, 0, 2)
        expo(0, 0)
        quant_half("q", 0, 1, 1)
        logits(1, 0, 1 + W[6])
        minpass(0, 1)
        untangle("q", 0, 2, s_copy)
        v_inter(s_copy, "vp", 0, 2, 4)
        expo(0, 1)
        v_inter(s_copy, "vp", 0, 3, 4)
        logits(1, 1, 1 + W[8])
        v_group("vn", 0)
        for label in ("vp", "vn"):
            v_group(label, 1)

        turns = {0: (("q", 0), ("q", 2), ("kp", 0)), 1: (("kp", 2), ("kn", 0), ("kn", 2))}
        sparts = {2: (0,), 3: (1,)}

        def side_turn(i, k):
            if i in turns:
                turn(turns[i][k][0], 1, turns[i][k][1])

        def side_copy(i, k):
            if i in turns:
                untangle(turns[i][k][0], 1, turns[i][k][1], s_copy)

        def side_quant(i, k):
            if i in turns:
                quant_half(turns[i][k][0], 1, turns[i][k][1])

        for i in range(PAIRS - 1):
            nxt, prev = i + 1, i - 1
            side_turn(i, 0)
            side_copy(i, 0)
            minpass(nxt, 0)
            if i == 0:
                quant_half("q", 0, 2)
            if i + 2 < PAIRS:
                logits(i + 2, 0, 1 + (W[10] if i >= 1 else W[11]))
            expo(nxt, 0)
            minpass(nxt, 1)
            if i + 2 < PAIRS and not W[15]:
                logits(i + 2, 1, 1 + W[12])
            side_turn(i, 1)
            if i == 1:
                side_turn(i, 2)
            expo(nxt, 1)
            side_copy(i, 1)
            if i == 0:
                v_quant("vp", 0)
            recip(i, 0, 3 if i >= 2 else 2)
            if i == 1:
                v_quant("vn", 0)
            if i == 5:
                v_quant("vn", 1)
            if i >= 2:
                clipped(i - 2, nc.vector)
            if prev >= 0:
                quant_probs(prev)
                values(prev)
            side_quant(i, 0)
            if i == 4:
                v_quant("vp", 1)
            probs(i, 0)
            if i >= 2:
                factor(i - 2)
            probs(i, 1)
            if i == 0:
                side_turn(i, 2)
            if i == 1:
                side_copy(i, 2)
            if prev >= 0:
                abs_sum(prev, "zp")
                abs_sum(prev, "zt")
                bound(prev)
            turn_probs(i)
            if i + 2 < PAIRS and W[15]:
                logits(i + 2, 1, 1 + W[14])
            side_quant(i, 1)
            if i == 0:
                side_copy(i, 2)
            copy_probs(i)
            if i == 0:
                v_inter(v_copy, "vn", 0, 0, 2)
                v_inter(s_copy, "vn", 0, 1, 2)
            if prev >= 0:
                norm(prev)
                keep_zp(prev, False)
            if i >= 2:
                blend(i - 2)
            if i >= W[9]:
                warm_mx(i, W[13])
            side_quant(i, 2)
            if i == 2:
                v_inter(v_copy, "vp", 1, 0, 1)
            if i == 4:
                v_inter(v_copy, "vn", 1, 1, 2)
            for part in sparts.get(i, ()):
                v_inter(s_copy, "vn", 1, part, 4)
            if i == 6:
                planes_group(0)
                planes_inter(0, 0, 256, v_copy)

        i = PAIRS - 1
        recip(i, 0, 2)
        probs(i, 0)
        turn_branch(i, 0)
        probs(i, 1)
        turn_branch(i, 1)
        quant_probs(i - 1)
        values(i - 1)
        recip(i, 2, 3)
        clipped(i - 2, nc.vector)
        copy_branch(i, 0, s_copy)
        factor(i - 2)
        copy_branch(i, 1, s_copy)
        quant_branch(i, 0)
        blend(i - 2)
        quant_branch(i, 1)
        abs_sum(i - 1, "zp")
        abs_sum(i - 1, "zt")
        keep_zp(i - 1, True)
        bound(i - 1)
        norm(i - 1)
        values(i)
        planes_inter(0, 256, D, v_copy)
        recip(i + 1, 2, 3)
        clipped(i - 1, nc.vector)
        factor(i - 1)
        planes_quant(0, 0, D)
        planes_store(0, 0, D)
        scales_store(0)
        blend(i - 1)
        abs_sum(i, "zp")
        keep_zp(i, True)
        bound(i)
        abs_sum(i, "zt")
        norm(i)
        clipped(i, nc.vector)
        recip(i + 2, 2, 3)
        factor(i)
        blend(i)
        planes_group(1)
        planes_inter(1, 0, 352, v_copy)
        planes_inter(1, 352, D, s_copy)
        planes_quant(1, 0, 256)
        planes_quant(1, 256, D)
        planes_store(1, 0, D)
        scales_store(1)
